import numpy as np
import ml_dtypes


def mxq(x, axis, fmt="e4m3"):
    dtype, down = {"e4m3": (ml_dtypes.float8_e4m3fn, 7), "e5m2": (ml_dtypes.float8_e5m2, 14)}[fmt]
    v = np.moveaxis(np.asarray(x, np.float32).astype(ml_dtypes.bfloat16).astype(np.float64), axis, -1)
    blocks = v.reshape(v.shape[:-1] + (-1, 32))
    amax = np.abs(blocks).max(-1, keepdims=True)
    byte = np.maximum(np.where(amax > 0, np.frexp(amax)[1] - 1 + 127, 0) - down, 1)
    scale = np.exp2(byte - 127.0)
    codes = (blocks / scale).astype(np.float32).astype(dtype).astype(np.float64)
    return np.moveaxis((codes * scale).reshape(v.shape), -1, axis)


WIDE = False


def mx_kscale(k):
    if not WIDE:
        return np.ones(k)
    levels = np.array([30, -30])
    if k % 512:
        return np.exp2(np.random.permutation(np.resize(levels, k // 32))).repeat(32)
    a = np.empty((k // 512, 16))
    for p in range(k // 512):
        a[p, :8] = np.random.permutation(np.resize(levels, 8))
        for g in range(8):
            far = levels[np.abs(levels - a[p, g]) >= 10]
            a[p, g + 8] = far[np.random.randint(len(far))]
    return np.exp2(a.ravel()).repeat(32)


def f64(x):
    return np.asarray(x).astype(np.float64)


def striped(idx):
    return np.tile(np.asarray(idx).reshape(-1, 16).T, (8, 1)).astype(np.uint16)


def unstriped(offs):
    return offs[:16].T.reshape(-1).astype(np.int64)


def striped8(idx):
    return np.asarray(idx).reshape(8, -1, 16).transpose(0, 2, 1).reshape(128, -1).astype(np.uint16)


def unstriped8(offs):
    return offs.reshape(8, 16, -1).transpose(0, 2, 1).reshape(8, -1).astype(np.int64)


def pick8(x, idx, run):
    r = np.arange(len(x))
    return x[r[:, None], idx[r % (8 * run) // run]]


E2M1 = np.array([0.0, 0.5, 1.0, 1.5, 2.0, 3.0, 4.0, 6.0, -0.0, -0.5, -1.0, -1.5, -2.0, -3.0, -4.0, -6.0])


def pack_weight(w, fmt):
    k, n = w.shape
    w = f64(np.asarray(w, np.float32).astype(ml_dtypes.bfloat16)).reshape(k // 32, 32, n)
    amax = np.abs(w).max(1)
    if fmt in ("e4m3", "e5m2"):
        byte = np.frexp(amax)[1] - 1 + 127 - (7 if fmt == "e4m3" else 14)
    else:
        mant, ex = np.frexp(amax / 6.0)
        byte = np.where(mant > 0.5, ex, ex - 1) + 127
    byte = np.clip(np.where(amax > 0, byte, 1), 1, 254)
    scaled = (w * np.exp2(127.0 - byte)[:, None, :]).reshape(k, n).astype(np.float32)
    by_word = np.ascontiguousarray(scaled.reshape(k // 512, 128, 4, n).transpose(0, 1, 3, 2))
    if fmt in ("e4m3", "e5m2"):
        words = by_word.astype(ml_dtypes.float8_e4m3fn if fmt == "e4m3" else ml_dtypes.float8_e5m2).view(np.uint8)
    else:
        c = by_word.astype(ml_dtypes.float4_e2m1fn).view(np.uint8) & 0xF
        words = (c[..., 0::2] | (c[..., 1::2] << 4)).reshape(k // 512, 128, 2 * n)
    return np.ascontiguousarray(words), np.ascontiguousarray(byte.astype(np.uint8).reshape(k // 512, 16, n))


def unpack_weight(words, scales, fmt):
    g, _, n = scales.shape
    words = np.ascontiguousarray(words).reshape(g, 128, n, -1)
    if fmt in ("e4m3", "e5m2"):
        vals = words.view(ml_dtypes.float8_e4m3fn if fmt == "e4m3" else ml_dtypes.float8_e5m2).astype(np.float64)
    else:
        nib = np.empty((g, 128, n, 4), np.uint8)
        nib[..., 0::2] = words & 0xF
        nib[..., 1::2] = words >> 4
        vals = E2M1[nib]
    vals = vals * np.repeat(np.exp2(scales.astype(np.float64) - 127.0), 8, axis=1)[..., None]
    return vals.transpose(0, 1, 3, 2).reshape(g * 512, n)


K, T, J, R, C, I, O, N, E = 512, 2048, 256, 512, 512, 128, 128, 256, 512


def setup_inputs():
    n = np.random.standard_normal
    idx = np.random.permutation(T)[:J]
    idx2 = np.random.permutation(T)[:J]
    idx3 = np.random.permutation(J)[:I]
    idx4 = np.stack([np.random.permutation(C)[:I] for _ in range(8)])
    idx5 = np.random.permutation(C)[:O]
    idx6 = np.random.permutation(J)[:O]
    idx7 = np.stack([np.random.permutation(E)[:O] for _ in range(8)])
    fk = mx_kscale(K)
    fr = mx_kscale(R)
    xtp = pack_weight(n((K, T)) / fk[:, None], "e5m2")
    wp = pack_weight(n((K, R)) * 1 / np.sqrt(K) * fk[:, None] * fr, "e2m1")
    w2p = pack_weight(n((K, R)) * 1 / np.sqrt(K) * fk[:, None] * fr, "e4m3")
    wbp = pack_weight(n((R, N)) * 1 / np.sqrt(R) / fr[:, None], "e2m1")
    return {
        "xt_words": xtp[0],
        "xt_scales": xtp[1],
        "w_words": wp[0],
        "w_scales": wp[1],
        "w2_words": w2p[0],
        "w2_scales": w2p[1],
        "sa": (np.random.uniform(0.5, 1.6, (R, 1))).astype(np.float32),
        "sb": (np.random.uniform(0.5, 1.6, (R, 1))).astype(np.float32),
        "wb_words": wbp[0],
        "wb_scales": wbp[1],
        "offs": striped(idx),
        "offs2": striped(idx2),
        "offs3": striped(idx3),
        "offs4": striped8(idx4),
        "offs5": striped(idx5),
        "offs6": striped(idx6),
        "offs7": striped8(idx7),
    }


def reference(xt_words, xt_scales, w_words, w_scales, w2_words, w2_scales, sa, sb, wb_words, wb_scales, offs, offs2, offs3, offs4, offs5, offs6, offs7):
    idx = unstriped(offs)
    idx2 = unstriped(offs2)
    idx3 = unstriped(offs3)
    idx4 = unstriped8(offs4)
    idx5 = unstriped(offs5)
    idx6 = unstriped(offs6)
    idx7 = unstriped8(offs7)
    xtu = unpack_weight(xt_words, xt_scales, "e5m2")
    wu = unpack_weight(w_words, w_scales, "e2m1")
    w2u = unpack_weight(w2_words, w2_scales, "e4m3")
    wbu = unpack_weight(wb_words, wb_scales, "e2m1")
    xtidxg = xtu[:, idx]
    a = wu.T @ xtidxg
    xtidx2g = xtu[:, idx2]
    b = w2u.T @ xtidx2g
    h1 = a[:, idx3] * f64(sa)
    pw = np.zeros((R, C))
    pw[np.arange(R)[:, None], idx4[np.arange(R) % 512 // 64]] = h1
    hid = np.abs(pw[:, idx5] - b[:, idx6] * f64(sb))
    hidq = mxq(hid, 0, "e4m3")
    p = wbu.T @ hidq
    y = np.zeros((N, E))
    y[np.arange(N)[:, None], idx7[np.arange(N) % 128 // 16]] = p
    return y

@@ -1,0 +1,202 @@
+from contextlib import ExitStack
+
+import concourse.mybir as mybir
+
+F32 = mybir.dt.float32
+BF16 = mybir.dt.bfloat16
+I32 = mybir.dt.int32
+U32 = mybir.dt.uint32
+U16 = mybir.dt.uint16
+U8 = mybir.dt.uint8
+E4M3 = mybir.dt.float8_e4m3fn_x4
+E5M2 = mybir.dt.float8_e5m2_x4
+E2M1 = mybir.dt.float4_e2m1fn_x4
+ACT = mybir.ActivationFunctionType
+ALU = mybir.AluOpType
+
+P = 128
+PACK = 4
+T, J, R, C, SEATS, PLACES, N, E = 2048, 256, 512, 512, 128, 128, 256, 512
+
+FLOPS = 2 * 512 * (2 * R * J + N * PLACES)
+
+
+def tile_list_ownseats_ahead_one_ownpage_kernel(
+    tc, xt_words, xt_scales, w_words, w_scales, w2_words, w2_scales, sa, sb, wb_words, wb_scales,
+    offs, offs2, offs3, offs4, offs5, offs6, offs7, out,
+):
+    nc = tc.nc
+    with ExitStack() as ctx:
+        pool = ctx.enter_context(tc.tile_pool(name="held", bufs=1))
+        psum = ctx.enter_context(tc.psum_pool(name="psum", bufs=8))
+
+        def tile(name, cols, dtype, rows=P):
+            return pool.tile([rows, cols], dtype, name=name, align_bytes=64)
+
+        def load_list(name, src):
+            lst = pool.tile(list(src.shape), U16, name=name)
+            nc.sync.dma_start(lst[:], src)
+            return lst
+
+        def zeroed_plane(name, cols):
+            plane = tile(name, cols, U8)
+            nc.vector.memset(plane[:].bitcast(I32), 0)
+            return plane
+
+        def load_staged(queue, name, scales, cols):
+            staged = tile(name, cols, I32, rows=4)
+            queue.dma_start(
+                staged[:].rearrange("r (q c) -> r q c", q=4),
+                scales[0].bitcast(I32).rearrange("(q r) c -> r q c", r=4),
+            )
+            return staged
+
+        def spread(plane, staged, cols):
+            words = cols // 4
+            for q in range(4):
+                nc.vector.tensor_copy(
+                    plane[32 * q : 32 * q + 4, :].bitcast(I32), staged[:, q * words : (q + 1) * words]
+                )
+
+        def deal(copy, dst, src, run):
+            copy(
+                dst.rearrange("p (t b i) -> p b t i", t=PACK, i=run),
+                src.rearrange("p (b i t) -> p b t i", t=PACK, i=run),
+            )
+
+        xs_plane = zeroed_plane("xs_plane", T)
+        l1 = load_list("l1", offs)
+        ws_staged = load_staged(nc.sync, "ws_staged", w_scales, R)
+        w_raw = tile("w_raw", 2 * R, U8)
+        nc.sync.dma_start(w_raw[:].bitcast(I32), w_words[0].bitcast(I32))
+        for r in range(4):
+            nc.scalar.dma_start(xs_plane[r:P:32, :].bitcast(I32), xt_scales[0, r:16:4, :].bitcast(I32))
+        l2 = load_list("l2", offs2)
+        l3 = load_list("l3", offs3)
+        xw = tile("xw", T, I32)
+        nc.sync.dma_start(xw[:], xt_words[0].rearrange("p n t -> p (n t)").bitcast(I32))
+        sa_t = tile("sa_t", PACK, F32)
+        nc.sync.dma_start(sa_t[:], sa.rearrange("(p t) o -> p (t o)", t=PACK))
+        w2_raw = tile("w2_raw", R, I32)
+        nc.sync.dma_start(w2_raw[:], w2_words[0].rearrange("p n t -> p (n t)").bitcast(I32))
+        w2s_staged = load_staged(nc.sync, "w2s_staged", w2_scales, R)
+        l4 = load_list("l4", offs4)
+        l6 = load_list("l6", offs6)
+        sb_t = tile("sb_t", PACK, F32)
+        nc.sync.dma_start(sb_t[:], sb.rearrange("(p t) o -> p (t o)", t=PACK))
+        l5 = load_list("l5", offs5)
+
+        ws_plane = zeroed_plane("ws_plane", R)
+        w2s_plane = zeroed_plane("w2s_plane", R)
+        wbs = zeroed_plane("wbs", N)
+        wb = tile("wb", 2 * N, U8)
+        nc.sync.dma_start(wb[:].bitcast(I32), wb_words[0].bitcast(I32))
+        for r in range(4):
+            nc.sync.dma_start(wbs[r:P:32, :].bitcast(I32), wb_scales[0, r:16:4, :].bitcast(I32))
+        l7 = load_list("l7", offs7)
+
+        w = tile("w", 2 * R, U8)
+        deal(nc.scalar.copy, w[:].bitcast(U16), w_raw[:].bitcast(U16), 8)
+        spread(ws_plane, ws_staged, R)
+        ws = tile("ws", R, U8)
+        deal(nc.vector.tensor_copy, ws[:], ws_plane[:], 16)
+        xs1 = tile("xs1", J, U8)
+        nc.vector.tensor_copy(xs1[:], xs_plane[:].indirect(l1[:]))
+        xs2 = tile("xs2", J, U8)
+        nc.vector.tensor_copy(xs2[:], xs_plane[:].indirect(l2[:]))
+        xw1 = tile("xw1", J, U32)
+        nc.vector.tensor_copy(xw1[:], xw[:].bitcast(U32).indirect(l1[:]))
+        xw2 = tile("xw2", J, U32)
+        nc.vector.tensor_copy(xw2[:], xw[:].bitcast(U32).indirect(l2[:]))
+
+
+        a = []
+        for t in range(PACK):
+            acc = psum.tile([P, J], F32, name="acc")
+            nc.tensor.matmul_mx(
+                acc[:],
+                lhsT=w[:, 2 * P * t : 2 * P * (t + 1)].bitcast(E2M1),
+                lhsT_scale=ws[:, P * t : P * (t + 1)],
+                rhs=xw1[:].bitcast(E5M2),
+                rhs_scale=xs1[:],
+                start=True,
+                stop=True,
+            )
+            a_t = tile("a%d" % t, J, F32)
+            nc.vector.tensor_copy(a_t[:], acc[:])
+            a.append(a_t)
+
+        board = [tile("board%d" % t, C, F32) for t in range(PACK)]
+        for t in range(PACK):
+            nc.vector.memset(board[t][:], 0.0)
+        seats = tile("seats", PACK * SEATS, F32)
+
+        def seat(t):
+            nc.scalar.activation(
+                seats[:, SEATS * t : SEATS * (t + 1)], a[t][:].indirect(l3[:]), ACT.Copy, scale=sa_t[:, t : t + 1]
+            )
+
+        def put(t):
+            nc.scalar.activation(board[t][:].indirect(l4[:]), seats[:, SEATS * t : SEATS * (t + 1)], ACT.Copy)
+
+        seat(0)
+        for t in range(1, PACK):
+            seat(t)
+            put(t - 1)
+        put(PACK - 1)
+
+        spread(w2s_plane, w2s_staged, R)
+        w2 = tile("w2", R, U32)
+        deal(nc.vector.tensor_copy, w2[:], w2_raw[:].bitcast(U32), 4)
+        w2s = tile("w2s", R, U8)
+        deal(nc.vector.tensor_copy, w2s[:], w2s_plane[:], 16)
+
+        second = tile("second", PACK * PLACES, F32)
+        diff = tile("diff", PACK * PLACES, F32)
+        for t in range(PACK):
+            acc = psum.tile([P, J], F32, name="acc")
+            nc.tensor.matmul_mx(
+                acc[:],
+                lhsT=w2[:, P * t : P * (t + 1)].bitcast(E4M3),
+                lhsT_scale=w2s[:, P * t : P * (t + 1)],
+                rhs=xw2[:].bitcast(E5M2),
+                rhs_scale=xs2[:],
+                start=True,
+                stop=True,
+            )
+            b_t = tile("b%d" % t, J, F32)
+            nc.vector.tensor_copy(b_t[:], acc[:])
+            cols = slice(PLACES * t, PLACES * (t + 1))
+            nc.scalar.activation(second[:, cols], b_t[:].indirect(l6[:]), ACT.Copy, scale=sb_t[:, t : t + 1])
+        for t in range(PACK):
+            cols = slice(PLACES * t, PLACES * (t + 1))
+            nc.vector.tensor_tensor(diff[:, cols], board[t][:].indirect(l5[:]), second[:, cols], ALU.subtract)
+
+        hid = tile("hid", PACK * PLACES, BF16)
+        nc.scalar.activation(
+            hid[:].rearrange("p (c i t) -> p c t i", t=PACK, i=4),
+            diff[:].rearrange("p (t c i) -> p c t i", t=PACK, i=4),
+            ACT.Abs,
+        )
+        hq = tile("hq", PLACES, U32)
+        hs = tile("hs", PLACES, U8)
+        nc.vector.quantize_mx(hq[:].bitcast(E4M3), hs[:], hid[:])
+
+        page = [tile("page%d" % h, E, F32) for h in range(N // P)]
+        for h in range(N // P):
+            nc.vector.memset(page[h][:], 0.0)
+        for h in range(N // P):
+            acc = psum.tile([P, J], F32, name="acc")
+            nc.tensor.matmul_mx(
+                acc[:, :PLACES],
+                lhsT=wb[:, 2 * P * h : 2 * P * (h + 1)].bitcast(E2M1),
+                lhsT_scale=wbs[:, P * h : P * (h + 1)],
+                rhs=hq[:].bitcast(E4M3),
+                rhs_scale=hs[:],
+                start=True,
+                stop=True,
+            )
+            res = tile("res%d" % h, PLACES, F32)
+            nc.vector.tensor_copy(res[:], acc[:, :PLACES])
+            nc.scalar.activation(page[h][:].indirect(l7[:]), res[:], ACT.Copy)
+            nc.sync.dma_start(out[P * h : P * (h + 1), :], page[h][:])

@@ -18,6 +18,8 @@ P = 128
 PACK = 4
 T, J, R, C, SEATS, PLACES, N, E = 2048, 256, 512, 512, 128, 128, 256, 512
 
+SPLIT = 80
+
 FLOPS = 2 * 512 * (2 * R * J + N * PLACES)
 
 
@@ -28,18 +30,18 @@ def tile_list_ownseats_ahead_one_ownpage_kernel(
     nc = tc.nc
     with ExitStack() as ctx:
         pool = ctx.enter_context(tc.tile_pool(name="held", bufs=1))
-        psum = ctx.enter_context(tc.psum_pool(name="psum", bufs=8))
+        psum = ctx.enter_context(tc.psum_pool(name="psum", bufs=1))
 
-        def tile(name, cols, dtype, rows=P):
-            return pool.tile([rows, cols], dtype, name=name, align_bytes=64)
+        def tile(name, cols, dtype, rows=P, tag=None):
+            return pool.tile([rows, cols], dtype, name=name, tag=tag or name, align_bytes=64)
 
         def load_list(name, src):
             lst = pool.tile(list(src.shape), U16, name=name)
             nc.sync.dma_start(lst[:], src)
             return lst
 
-        def zeroed_plane(name, cols):
-            plane = tile(name, cols, U8)
+        def zeroed_plane(name, cols, tag=None):
+            plane = tile(name, cols, U8, tag=tag)
             nc.vector.memset(plane[:].bitcast(I32), 0)
             return plane
 
@@ -66,20 +68,20 @@ def tile_list_ownseats_ahead_one_ownpage_kernel(
 
         xs_plane = zeroed_plane("xs_plane", T)
         l1 = load_list("l1", offs)
-        ws_staged = load_staged(nc.sync, "ws_staged", w_scales, R)
         w_raw = tile("w_raw", 2 * R, U8)
-        nc.sync.dma_start(w_raw[:].bitcast(I32), w_words[0].bitcast(I32))
+        nc.scalar.dma_start(w_raw[:].bitcast(I32), w_words[0].bitcast(I32))
+        ws_staged = load_staged(nc.sync, "ws_staged", w_scales, R)
+        xw = tile("xw", T, I32)
+        nc.scalar.dma_start(xw[:], xt_words[0].rearrange("p n t -> p (n t)").bitcast(I32))
         for r in range(4):
-            nc.scalar.dma_start(xs_plane[r:P:32, :].bitcast(I32), xt_scales[0, r:16:4, :].bitcast(I32))
+            nc.sync.dma_start(xs_plane[r:P:32, :].bitcast(I32), xt_scales[0, r:16:4, :].bitcast(I32))
         l2 = load_list("l2", offs2)
         l3 = load_list("l3", offs3)
-        xw = tile("xw", T, I32)
-        nc.sync.dma_start(xw[:], xt_words[0].rearrange("p n t -> p (n t)").bitcast(I32))
         sa_t = tile("sa_t", PACK, F32)
         nc.sync.dma_start(sa_t[:], sa.rearrange("(p t) o -> p (t o)", t=PACK))
-        w2_raw = tile("w2_raw", R, I32)
-        nc.sync.dma_start(w2_raw[:], w2_words[0].rearrange("p n t -> p (n t)").bitcast(I32))
         w2s_staged = load_staged(nc.sync, "w2s_staged", w2_scales, R)
+        w2_raw = tile("w2_raw", R, I32, tag="late0")
+        nc.sync.dma_start(w2_raw[:], w2_words[0].rearrange("p n t -> p (n t)").bitcast(I32))
         l4 = load_list("l4", offs4)
         l6 = load_list("l6", offs6)
         sb_t = tile("sb_t", PACK, F32)
@@ -87,7 +89,7 @@ def tile_list_ownseats_ahead_one_ownpage_kernel(
         l5 = load_list("l5", offs5)
 
         ws_plane = zeroed_plane("ws_plane", R)
-        w2s_plane = zeroed_plane("w2s_plane", R)
+        w2s_plane = zeroed_plane("w2s_plane", R, tag="late1")
         wbs = zeroed_plane("wbs", N)
         wb = tile("wb", 2 * N, U8)
         nc.sync.dma_start(wb[:].bitcast(I32), wb_words[0].bitcast(I32))
@@ -110,83 +112,97 @@ def tile_list_ownseats_ahead_one_ownpage_kernel(
         nc.vector.tensor_copy(xw2[:], xw[:].bitcast(U32).indirect(l2[:]))
 
 
-        a = []
-        for t in range(PACK):
-            acc = psum.tile([P, J], F32, name="acc")
+        def product(name, bank, words, scales, tokens, token_scales, copy):
+            acc = psum.tile([P, J], F32, name="acc", tag="bank%d" % bank)
             nc.tensor.matmul_mx(
-                acc[:],
-                lhsT=w[:, 2 * P * t : 2 * P * (t + 1)].bitcast(E2M1),
-                lhsT_scale=ws[:, P * t : P * (t + 1)],
-                rhs=xw1[:].bitcast(E5M2),
-                rhs_scale=xs1[:],
-                start=True,
-                stop=True,
+                acc[:], lhsT=words, lhsT_scale=scales, rhs=tokens[:].bitcast(E5M2), rhs_scale=token_scales[:],
+                start=True, stop=True,
             )
-            a_t = tile("a%d" % t, J, F32)
-            nc.vector.tensor_copy(a_t[:], acc[:])
-            a.append(a_t)
+            rows = tile(name, J, F32)
+            copy(rows[:], acc[:])
+            return rows
+
+        def first(t, bank, copy=nc.vector.tensor_copy):
+            words = w[:, 2 * P * t : 2 * P * (t + 1)].bitcast(E2M1)
+            return product("a%d" % t, bank, words, ws[:, P * t : P * (t + 1)], xw1, xs1, copy)
+
+        def second(t, bank):
+            words = w2[:, P * t : P * (t + 1)].bitcast(E4M3)
+            return product("b%d" % t, bank, words, w2s[:, P * t : P * (t + 1)], xw2, xs2, nc.vector.tensor_copy)
 
         board = [tile("board%d" % t, C, F32) for t in range(PACK)]
-        for t in range(PACK):
-            nc.vector.memset(board[t][:], 0.0)
         seats = tile("seats", PACK * SEATS, F32)
+        weighted = tile("weighted", PACK * PLACES, F32)
+        diff = tile("diff", PACK * PLACES, F32)
 
-        def seat(t):
+        def seat(t, rows):
             nc.scalar.activation(
-                seats[:, SEATS * t : SEATS * (t + 1)], a[t][:].indirect(l3[:]), ACT.Copy, scale=sa_t[:, t : t + 1]
+                seats[:, SEATS * t : SEATS * (t + 1)], rows[:].indirect(l3[:]), ACT.Copy, scale=sa_t[:, t : t + 1]
             )
 
         def put(t):
             nc.scalar.activation(board[t][:].indirect(l4[:]), seats[:, SEATS * t : SEATS * (t + 1)], ACT.Copy)
 
-        seat(0)
-        for t in range(1, PACK):
-            seat(t)
+        def weigh(t, rows):
+            nc.scalar.activation(
+                weighted[:, PLACES * t : PLACES * (t + 1)], rows[:].indirect(l6[:]), ACT.Copy, scale=sb_t[:, t : t + 1]
+            )
+
+        def differ(t):
+            cols = slice(PLACES * t, PLACES * (t + 1))
+            nc.vector.tensor_tensor(diff[:, cols], board[t][:].indirect(l5[:]), weighted[:, cols], ALU.subtract)
+
+        last = PACK - 1
+        a = [first(0, 0, nc.scalar.copy)] + [first(t, t) for t in range(1, last)]
+        for t in range(PACK):
+            nc.vector.memset(board[t][:].bitcast(I32), 0)
+        seat(0, a[0])
+        for t in range(1, last):
+            seat(t, a[t])
             put(t - 1)
-        put(PACK - 1)
+        put(last - 1)
 
         spread(w2s_plane, w2s_staged, R)
-        w2 = tile("w2", R, U32)
-        deal(nc.vector.tensor_copy, w2[:], w2_raw[:].bitcast(U32), 4)
         w2s = tile("w2s", R, U8)
         deal(nc.vector.tensor_copy, w2s[:], w2s_plane[:], 16)
+        w2 = tile("w2", R, U32)
+        deal(nc.vector.tensor_copy, w2[:], w2_raw[:].bitcast(U32), 4)
 
-        second = tile("second", PACK * PLACES, F32)
-        diff = tile("diff", PACK * PLACES, F32)
-        for t in range(PACK):
-            acc = psum.tile([P, J], F32, name="acc")
-            nc.tensor.matmul_mx(
-                acc[:],
-                lhsT=w2[:, P * t : P * (t + 1)].bitcast(E4M3),
-                lhsT_scale=w2s[:, P * t : P * (t + 1)],
-                rhs=xw2[:].bitcast(E5M2),
-                rhs_scale=xs2[:],
-                start=True,
-                stop=True,
-            )
-            b_t = tile("b%d" % t, J, F32)
-            nc.vector.tensor_copy(b_t[:], acc[:])
-            cols = slice(PLACES * t, PLACES * (t + 1))
-            nc.scalar.activation(second[:, cols], b_t[:].indirect(l6[:]), ACT.Copy, scale=sb_t[:, t : t + 1])
-        for t in range(PACK):
-            cols = slice(PLACES * t, PLACES * (t + 1))
-            nc.vector.tensor_tensor(diff[:, cols], board[t][:].indirect(l5[:]), second[:, cols], ALU.subtract)
+        b = [second(t, last + t) for t in range(2)]
+        a_last = first(last, last)
+        b = b + [second(t, last + t) for t in range(2, PACK)]
+        weigh(0, b[0])
+        weigh(1, b[1])
+        seat(last, a_last)
+        weigh(2, b[2])
+        put(last)
+        weigh(last, b[last])
+        for t in range(last):
+            differ(t)
+        picked = tile("picked", PLACES, F32)
+        nc.vector.tensor_copy(picked[:], board[last][:].indirect(l5[:]))
+        nc.vector.tensor_tensor(diff[:, PLACES * last :], picked[:], weighted[:, PLACES * last :], ALU.subtract)
 
         hid = tile("hid", PACK * PLACES, BF16)
+        by_row = diff[:].rearrange("p (t o) -> p t o", t=PACK)
         nc.scalar.activation(
-            hid[:].rearrange("p (c i t) -> p c t i", t=PACK, i=4),
-            diff[:].rearrange("p (t c i) -> p c t i", t=PACK, i=4),
+            hid[:, : PACK * SPLIT].rearrange("p (c i t) -> p c t i", t=PACK, i=4),
+            by_row[:, :, :SPLIT].rearrange("p t (c i) -> p c t i", i=4),
             ACT.Abs,
+        )
+        rest = by_row[:, :, SPLIT:].rearrange("p t o -> p o t")
+        nc.vector.scalar_tensor_tensor(
+            hid[:, PACK * SPLIT :].rearrange("p (o t) -> p o t", t=PACK), rest, -1.0, rest, ALU.mult, ALU.max
         )
         hq = tile("hq", PLACES, U32)
         hs = tile("hs", PLACES, U8)
         nc.vector.quantize_mx(hq[:].bitcast(E4M3), hs[:], hid[:])
 
-        page = [tile("page%d" % h, E, F32) for h in range(N // P)]
+        page = [tile("page%d" % h, E, F32, tag="late%d" % h) for h in range(N // P)]
         for h in range(N // P):
-            nc.vector.memset(page[h][:], 0.0)
+            nc.gpsimd.memset(page[h][:], 0.0)
         for h in range(N // P):
-            acc = psum.tile([P, J], F32, name="acc")
+            acc = psum.tile([P, J], F32, name="acc", tag="bank%d" % h)
             nc.tensor.matmul_mx(
                 acc[:, :PLACES],
                 lhsT=wb[:, 2 * P * h : 2 * P * (h + 1)].bitcast(E2M1),

@@ -18,7 +18,7 @@ P = 128
 PACK = 4
 T, J, R, C, SEATS, PLACES, N, E = 2048, 256, 512, 512, 128, 128, 256, 512
 
-SPLIT = 80
+SPLIT = 96
 
 FLOPS = 2 * 512 * (2 * R * J + N * PLACES)
 
@@ -68,19 +68,19 @@ def tile_list_ownseats_ahead_one_ownpage_kernel(
 
         xs_plane = zeroed_plane("xs_plane", T)
         l1 = load_list("l1", offs)
-        w_raw = tile("w_raw", 2 * R, U8)
-        nc.scalar.dma_start(w_raw[:].bitcast(I32), w_words[0].bitcast(I32))
         ws_staged = load_staged(nc.sync, "ws_staged", w_scales, R)
-        xw = tile("xw", T, I32)
-        nc.scalar.dma_start(xw[:], xt_words[0].rearrange("p n t -> p (n t)").bitcast(I32))
+        w_raw = tile("w_raw", 2 * R, U8)
+        nc.sync.dma_start(w_raw[:].bitcast(I32), w_words[0].bitcast(I32))
         for r in range(4):
             nc.sync.dma_start(xs_plane[r:P:32, :].bitcast(I32), xt_scales[0, r:16:4, :].bitcast(I32))
+        xw = tile("xw", T, I32)
+        nc.sync.dma_start(xw[:], xt_words[0].rearrange("p n t -> p (n t)").bitcast(I32))
         l2 = load_list("l2", offs2)
         l3 = load_list("l3", offs3)
         sa_t = tile("sa_t", PACK, F32)
         nc.sync.dma_start(sa_t[:], sa.rearrange("(p t) o -> p (t o)", t=PACK))
         w2s_staged = load_staged(nc.sync, "w2s_staged", w2_scales, R)
-        w2_raw = tile("w2_raw", R, I32, tag="late0")
+        w2_raw = tile("w2_raw", R, I32)
         nc.sync.dma_start(w2_raw[:], w2_words[0].rearrange("p n t -> p (n t)").bitcast(I32))
         l4 = load_list("l4", offs4)
         l6 = load_list("l6", offs6)
@@ -89,7 +89,7 @@ def tile_list_ownseats_ahead_one_ownpage_kernel(
         l5 = load_list("l5", offs5)
 
         ws_plane = zeroed_plane("ws_plane", R)
-        w2s_plane = zeroed_plane("w2s_plane", R, tag="late1")
+        w2s_plane = zeroed_plane("w2s_plane", R)
         wbs = zeroed_plane("wbs", N)
         wb = tile("wb", 2 * N, U8)
         nc.sync.dma_start(wb[:].bitcast(I32), wb_words[0].bitcast(I32))
@@ -104,8 +104,6 @@ def tile_list_ownseats_ahead_one_ownpage_kernel(
         deal(nc.vector.tensor_copy, ws[:], ws_plane[:], 16)
         xs1 = tile("xs1", J, U8)
         nc.vector.tensor_copy(xs1[:], xs_plane[:].indirect(l1[:]))
-        xs2 = tile("xs2", J, U8)
-        nc.vector.tensor_copy(xs2[:], xs_plane[:].indirect(l2[:]))
         xw1 = tile("xw1", J, U32)
         nc.vector.tensor_copy(xw1[:], xw[:].bitcast(U32).indirect(l1[:]))
         xw2 = tile("xw2", J, U32)
@@ -162,6 +160,8 @@ def tile_list_ownseats_ahead_one_ownpage_kernel(
             put(t - 1)
         put(last - 1)
 
+        xs2 = tile("xs2", J, U8)
+        nc.vector.tensor_copy(xs2[:], xs_plane[:].indirect(l2[:]))
         spread(w2s_plane, w2s_staged, R)
         w2s = tile("w2s", R, U8)
         deal(nc.vector.tensor_copy, w2s[:], w2s_plane[:], 16)
@@ -198,9 +198,9 @@ def tile_list_ownseats_ahead_one_ownpage_kernel(
         hs = tile("hs", PLACES, U8)
         nc.vector.quantize_mx(hq[:].bitcast(E4M3), hs[:], hid[:])
 
-        page = [tile("page%d" % h, E, F32, tag="late%d" % h) for h in range(N // P)]
+        page = [tile("page%d" % h, E, F32) for h in range(N // P)]
         for h in range(N // P):
-            nc.gpsimd.memset(page[h][:], 0.0)
+            nc.vector.memset(page[h][:].bitcast(I32), 0)
         for h in range(N // P):
             acc = psum.tile([P, J], F32, name="acc", tag="bank%d" % h)
             nc.tensor.matmul_mx(

@@ -18,8 +18,6 @@ P = 128
 PACK = 4
 T, J, R, C, SEATS, PLACES, N, E = 2048, 256, 512, 512, 128, 128, 256, 512
 
-SPLIT = 96
-
 FLOPS = 2 * 512 * (2 * R * J + N * PLACES)
 
 
@@ -79,17 +77,18 @@ def tile_list_ownseats_ahead_one_ownpage_kernel(
         l3 = load_list("l3", offs3)
         sa_t = tile("sa_t", PACK, F32)
         nc.sync.dma_start(sa_t[:], sa.rearrange("(p t) o -> p (t o)", t=PACK))
-        w2s_staged = load_staged(nc.sync, "w2s_staged", w2_scales, R)
         w2_raw = tile("w2_raw", R, I32)
         nc.sync.dma_start(w2_raw[:], w2_words[0].rearrange("p n t -> p (n t)").bitcast(I32))
         l4 = load_list("l4", offs4)
+        ws_plane = zeroed_plane("ws_plane", R)
+        w2s_plane = zeroed_plane("w2s_plane", R)
+        for r in range(4):
+            nc.sync.dma_start(w2s_plane[r:P:32, :].bitcast(I32), w2_scales[0, r:16:4, :].bitcast(I32))
         l6 = load_list("l6", offs6)
         sb_t = tile("sb_t", PACK, F32)
         nc.sync.dma_start(sb_t[:], sb.rearrange("(p t) o -> p (t o)", t=PACK))
         l5 = load_list("l5", offs5)
 
-        ws_plane = zeroed_plane("ws_plane", R)
-        w2s_plane = zeroed_plane("w2s_plane", R)
         wbs = zeroed_plane("wbs", N)
         wb = tile("wb", 2 * N, U8)
         nc.sync.dma_start(wb[:].bitcast(I32), wb_words[0].bitcast(I32))
@@ -146,61 +145,44 @@ def tile_list_ownseats_ahead_one_ownpage_kernel(
                 weighted[:, PLACES * t : PLACES * (t + 1)], rows[:].indirect(l6[:]), ACT.Copy, scale=sb_t[:, t : t + 1]
             )
 
-        def differ(t):
-            cols = slice(PLACES * t, PLACES * (t + 1))
-            nc.vector.tensor_tensor(diff[:, cols], board[t][:].indirect(l5[:]), weighted[:, cols], ALU.subtract)
-
-        last = PACK - 1
-        a = [first(0, 0, nc.scalar.copy)] + [first(t, t) for t in range(1, last)]
+        a = [first(0, 0, nc.scalar.copy)] + [first(t, t) for t in range(1, PACK)]
         for t in range(PACK):
             nc.vector.memset(board[t][:].bitcast(I32), 0)
         seat(0, a[0])
-        for t in range(1, last):
+        for t in range(1, PACK):
             seat(t, a[t])
             put(t - 1)
-        put(last - 1)
+        put(PACK - 1)
 
         xs2 = tile("xs2", J, U8)
         nc.vector.tensor_copy(xs2[:], xs_plane[:].indirect(l2[:]))
-        spread(w2s_plane, w2s_staged, R)
-        w2s = tile("w2s", R, U8)
-        deal(nc.vector.tensor_copy, w2s[:], w2s_plane[:], 16)
         w2 = tile("w2", R, U32)
         deal(nc.vector.tensor_copy, w2[:], w2_raw[:].bitcast(U32), 4)
+        w2s = tile("w2s", R, U8)
+        deal(nc.vector.tensor_copy, w2s[:], w2s_plane[:], 16)
 
-        b = [second(t, last + t) for t in range(2)]
-        a_last = first(last, last)
-        b = b + [second(t, last + t) for t in range(2, PACK)]
-        weigh(0, b[0])
-        weigh(1, b[1])
-        seat(last, a_last)
-        weigh(2, b[2])
-        put(last)
-        weigh(last, b[last])
-        for t in range(last):
-            differ(t)
-        picked = tile("picked", PLACES, F32)
-        nc.vector.tensor_copy(picked[:], board[last][:].indirect(l5[:]))
-        nc.vector.tensor_tensor(diff[:, PLACES * last :], picked[:], weighted[:, PLACES * last :], ALU.subtract)
+        for t in range(PACK):
+            weigh(t, second(t, PACK + t))
+        picked = tile("picked", PACK * PLACES, F32, tag="w2")
+        for t in range(PACK):
+            nc.vector.tensor_copy(picked[:, PLACES * t : PLACES * (t + 1)], board[t][:].indirect(l5[:]))
+        for t in range(PACK):
+            cols = slice(PLACES * t, PLACES * (t + 1))
+            nc.vector.tensor_tensor(diff[:, cols], picked[:, cols], weighted[:, cols], ALU.subtract)
 
         hid = tile("hid", PACK * PLACES, BF16)
-        by_row = diff[:].rearrange("p (t o) -> p t o", t=PACK)
         nc.scalar.activation(
-            hid[:, : PACK * SPLIT].rearrange("p (c i t) -> p c t i", t=PACK, i=4),
-            by_row[:, :, :SPLIT].rearrange("p t (c i) -> p c t i", i=4),
+            hid[:].rearrange("p (c i t) -> p c t i", t=PACK, i=4),
+            diff[:].rearrange("p (t c i) -> p c t i", t=PACK, i=4),
             ACT.Abs,
-        )
-        rest = by_row[:, :, SPLIT:].rearrange("p t o -> p o t")
-        nc.vector.scalar_tensor_tensor(
-            hid[:, PACK * SPLIT :].rearrange("p (o t) -> p o t", t=PACK), rest, -1.0, rest, ALU.mult, ALU.max
         )
         hq = tile("hq", PLACES, U32)
         hs = tile("hs", PLACES, U8)
         nc.vector.quantize_mx(hq[:].bitcast(E4M3), hs[:], hid[:])
 
-        page = [tile("page%d" % h, E, F32) for h in range(N // P)]
+        page = [tile("page%d" % h, E, F32, tag="a%d" % h) for h in range(N // P)]
         for h in range(N // P):
-            nc.vector.memset(page[h][:].bitcast(I32), 0)
+            nc.gpsimd.memset(page[h][:], 0.0)
         for h in range(N // P):
             acc = psum.tile([P, J], F32, name="acc", tag="bank%d" % h)
             nc.tensor.matmul_mx(

from contextlib import ExitStack

import concourse.mybir as mybir

F32 = mybir.dt.float32
BF16 = mybir.dt.bfloat16
I32 = mybir.dt.int32
U32 = mybir.dt.uint32
U16 = mybir.dt.uint16
U8 = mybir.dt.uint8
E4M3 = mybir.dt.float8_e4m3fn_x4
E5M2 = mybir.dt.float8_e5m2_x4
E2M1 = mybir.dt.float4_e2m1fn_x4
ACT = mybir.ActivationFunctionType
ALU = mybir.AluOpType

P = 128
PACK = 4
T, J, R, C, SEATS, PLACES, N, E = 2048, 256, 512, 512, 128, 128, 256, 512

FLOPS = 2 * 512 * (2 * R * J + N * PLACES)


def tile_list_ownseats_ahead_one_ownpage_kernel(
    tc, xt_words, xt_scales, w_words, w_scales, w2_words, w2_scales, sa, sb, wb_words, wb_scales,
    offs, offs2, offs3, offs4, offs5, offs6, offs7, out,
):
    nc = tc.nc
    with ExitStack() as ctx:
        pool = ctx.enter_context(tc.tile_pool(name="held", bufs=1))
        psum = ctx.enter_context(tc.psum_pool(name="psum", bufs=1))

        def tile(name, cols, dtype, rows=P, tag=None):
            return pool.tile([rows, cols], dtype, name=name, tag=tag or name, align_bytes=64)

        def load_list(name, src):
            lst = pool.tile(list(src.shape), U16, name=name)
            nc.sync.dma_start(lst[:], src)
            return lst

        def zeroed_plane(name, cols, tag=None):
            plane = tile(name, cols, U8, tag=tag)
            nc.vector.memset(plane[:].bitcast(I32), 0)
            return plane

        def load_staged(queue, name, scales, cols):
            staged = tile(name, cols, I32, rows=4)
            queue.dma_start(
                staged[:].rearrange("r (q c) -> r q c", q=4),
                scales[0].bitcast(I32).rearrange("(q r) c -> r q c", r=4),
            )
            return staged

        def spread(plane, staged, cols):
            words = cols // 4
            for q in range(4):
                nc.vector.tensor_copy(
                    plane[32 * q : 32 * q + 4, :].bitcast(I32), staged[:, q * words : (q + 1) * words]
                )

        def deal(copy, dst, src, run):
            copy(
                dst.rearrange("p (t b i) -> p b t i", t=PACK, i=run),
                src.rearrange("p (b i t) -> p b t i", t=PACK, i=run),
            )

        xs_plane = zeroed_plane("xs_plane", T)
        l1 = load_list("l1", offs)
        ws_staged = load_staged(nc.sync, "ws_staged", w_scales, R)
        w_raw = tile("w_raw", 2 * R, U8)
        nc.sync.dma_start(w_raw[:].bitcast(I32), w_words[0].bitcast(I32))
        for r in range(4):
            nc.sync.dma_start(xs_plane[r:P:32, :].bitcast(I32), xt_scales[0, r:16:4, :].bitcast(I32))
        xw = tile("xw", T, I32)
        nc.sync.dma_start(xw[:], xt_words[0].rearrange("p n t -> p (n t)").bitcast(I32))
        l2 = load_list("l2", offs2)
        l3 = load_list("l3", offs3)
        sa_t = tile("sa_t", PACK, F32)
        nc.sync.dma_start(sa_t[:], sa.rearrange("(p t) o -> p (t o)", t=PACK))
        w2_raw = tile("w2_raw", R, I32)
        nc.sync.dma_start(w2_raw[:], w2_words[0].rearrange("p n t -> p (n t)").bitcast(I32))
        l4 = load_list("l4", offs4)
        ws_plane = zeroed_plane("ws_plane", R)
        w2s_plane = zeroed_plane("w2s_plane", R)
        for r in range(4):
            nc.sync.dma_start(w2s_plane[r:P:32, :].bitcast(I32), w2_scales[0, r:16:4, :].bitcast(I32))
        l6 = load_list("l6", offs6)
        sb_t = tile("sb_t", PACK, F32)
        nc.sync.dma_start(sb_t[:], sb.rearrange("(p t) o -> p (t o)", t=PACK))
        l5 = load_list("l5", offs5)

        wbs = zeroed_plane("wbs", N)
        wb = tile("wb", 2 * N, U8)
        nc.sync.dma_start(wb[:].bitcast(I32), wb_words[0].bitcast(I32))
        for r in range(4):
            nc.sync.dma_start(wbs[r:P:32, :].bitcast(I32), wb_scales[0, r:16:4, :].bitcast(I32))
        l7 = load_list("l7", offs7)

        w = tile("w", 2 * R, U8)
        deal(nc.scalar.copy, w[:].bitcast(U16), w_raw[:].bitcast(U16), 8)
        spread(ws_plane, ws_staged, R)
        ws = tile("ws", R, U8)
        deal(nc.vector.tensor_copy, ws[:], ws_plane[:], 16)
        xs1 = tile("xs1", J, U8)
        nc.vector.tensor_copy(xs1[:], xs_plane[:].indirect(l1[:]))
        xw1 = tile("xw1", J, U32)
        nc.vector.tensor_copy(xw1[:], xw[:].bitcast(U32).indirect(l1[:]))
        xw2 = tile("xw2", J, U32)
        nc.vector.tensor_copy(xw2[:], xw[:].bitcast(U32).indirect(l2[:]))


        def product(name, bank, words, scales, tokens, token_scales, copy):
            acc = psum.tile([P, J], F32, name="acc", tag="bank%d" % bank)
            nc.tensor.matmul_mx(
                acc[:], lhsT=words, lhsT_scale=scales, rhs=tokens[:].bitcast(E5M2), rhs_scale=token_scales[:],
                start=True, stop=True,
            )
            rows = tile(name, J, F32)
            copy(rows[:], acc[:])
            return rows

        def first(t, bank, copy=nc.vector.tensor_copy):
            words = w[:, 2 * P * t : 2 * P * (t + 1)].bitcast(E2M1)
            return product("a%d" % t, bank, words, ws[:, P * t : P * (t + 1)], xw1, xs1, copy)

        def second(t, bank):
            words = w2[:, P * t : P * (t + 1)].bitcast(E4M3)
            return product("b%d" % t, bank, words, w2s[:, P * t : P * (t + 1)], xw2, xs2, nc.vector.tensor_copy)

        board = [tile("board%d" % t, C, F32) for t in range(PACK)]
        seats = tile("seats", PACK * SEATS, F32)
        weighted = tile("weighted", PACK * PLACES, F32)
        diff = tile("diff", PACK * PLACES, F32)

        def seat(t, rows):
            nc.scalar.activation(
                seats[:, SEATS * t : SEATS * (t + 1)], rows[:].indirect(l3[:]), ACT.Copy, scale=sa_t[:, t : t + 1]
            )

        def put(t):
            nc.scalar.activation(board[t][:].indirect(l4[:]), seats[:, SEATS * t : SEATS * (t + 1)], ACT.Copy)

        def weigh(t, rows):
            nc.scalar.activation(
                weighted[:, PLACES * t : PLACES * (t + 1)], rows[:].indirect(l6[:]), ACT.Copy, scale=sb_t[:, t : t + 1]
            )

        a = [first(0, 0, nc.scalar.copy)] + [first(t, t) for t in range(1, PACK)]
        for t in range(PACK):
            nc.vector.memset(board[t][:].bitcast(I32), 0)
        seat(0, a[0])
        for t in range(1, PACK):
            seat(t, a[t])
            put(t - 1)
        put(PACK - 1)

        xs2 = tile("xs2", J, U8)
        nc.vector.tensor_copy(xs2[:], xs_plane[:].indirect(l2[:]))
        w2 = tile("w2", R, U32)
        deal(nc.vector.tensor_copy, w2[:], w2_raw[:].bitcast(U32), 4)
        w2s = tile("w2s", R, U8)
        deal(nc.vector.tensor_copy, w2s[:], w2s_plane[:], 16)

        for t in range(PACK):
            weigh(t, second(t, PACK + t))
        picked = tile("picked", PACK * PLACES, F32, tag="w2")
        for t in range(PACK):
            nc.vector.tensor_copy(picked[:, PLACES * t : PLACES * (t + 1)], board[t][:].indirect(l5[:]))
        for t in range(PACK):
            cols = slice(PLACES * t, PLACES * (t + 1))
            nc.vector.tensor_tensor(diff[:, cols], picked[:, cols], weighted[:, cols], ALU.subtract)

        hid = tile("hid", PACK * PLACES, BF16)
        nc.scalar.activation(
            hid[:].rearrange("p (c i t) -> p c t i", t=PACK, i=4),
            diff[:].rearrange("p (t c i) -> p c t i", t=PACK, i=4),
            ACT.Abs,
        )
        hq = tile("hq", PLACES, U32)
        hs = tile("hs", PLACES, U8)
        nc.vector.quantize_mx(hq[:].bitcast(E4M3), hs[:], hid[:])

        page = [tile("page%d" % h, E, F32, tag="a%d" % h) for h in range(N // P)]
        for h in range(N // P):
            nc.gpsimd.memset(page[h][:], 0.0)
        for h in range(N // P):
            acc = psum.tile([P, J], F32, name="acc", tag="bank%d" % h)
            nc.tensor.matmul_mx(
                acc[:, :PLACES],
                lhsT=wb[:, 2 * P * h : 2 * P * (h + 1)].bitcast(E2M1),
                lhsT_scale=wbs[:, P * h : P * (h + 1)],
                rhs=hq[:].bitcast(E4M3),
                rhs_scale=hs[:],
                start=True,
                stop=True,
            )
            res = tile("res%d" % h, PLACES, F32)
            nc.vector.tensor_copy(res[:], acc[:, :PLACES])
            nc.scalar.activation(page[h][:].indirect(l7[:]), res[:], ACT.Copy)
            nc.sync.dma_start(out[P * h : P * (h + 1), :], page[h][:])
